import numpy as np
import ml_dtypes


def mxq(x, axis, fmt="e4m3"):
    dtype, down = {"e4m3": (ml_dtypes.float8_e4m3fn, 7), "e5m2": (ml_dtypes.float8_e5m2, 14)}[fmt]
    v = np.moveaxis(np.asarray(x, np.float32).astype(ml_dtypes.bfloat16).astype(np.float64), axis, -1)
    blocks = v.reshape(v.shape[:-1] + (-1, 32))
    amax = np.abs(blocks).max(-1, keepdims=True)
    byte = np.maximum(np.where(amax > 0, np.frexp(amax)[1] - 1 + 127, 0) - down, 1)
    scale = np.exp2(byte - 127.0)
    codes = (blocks / scale).astype(np.float32).astype(dtype).astype(np.float64)
    return np.moveaxis((codes * scale).reshape(v.shape), -1, axis)


WIDE = False


def mx_kscale(k):
    if not WIDE:
        return np.ones(k)
    levels = np.array([10, -10, 5, -5, 0])
    if k % 512:
        return np.exp2(np.random.permutation(np.resize(levels, k // 32))).repeat(32)
    a = np.empty((k // 512, 16))
    for p in range(k // 512):
        a[p, :8] = np.random.permutation(np.resize(levels, 8))
        for g in range(8):
            far = levels[np.abs(levels - a[p, g]) >= 10]
            a[p, g + 8] = far[np.random.randint(len(far))]
    return np.exp2(a.ravel()).repeat(32)


def f64(x):
    return np.asarray(x).astype(np.float64)


def striped(idx):
    return np.tile(idx.reshape(-1, 16).T, (8, 1)).astype(np.uint16)


def unstriped(offs):
    return offs[:16].T.reshape(-1).astype(np.int64)


def striped8(idx):
    return np.concatenate([x.reshape(-1, 16).T for x in idx]).astype(np.uint16)


def runs(offs, k):
    lists = np.stack([offs[16 * r : 16 * r + 16].T.reshape(-1) for r in range(8)]).astype(np.int64)
    return lists[np.arange(k) % 512 // 64]


def pack_weight(w):
    k, n = w.shape
    w = f64(np.asarray(w, np.float32).astype(ml_dtypes.bfloat16)).reshape(k // 32, 32, n)
    amax = np.abs(w).max(1)
    byte = np.clip(np.where(amax > 0, np.frexp(amax)[1] - 1 + 127 - 7, 1), 1, 254)
    scaled = (w * np.exp2(127.0 - byte)[:, None, :]).reshape(k, n).astype(np.float32)
    words = np.ascontiguousarray(scaled.reshape(k // 512, 128, 4, n).transpose(0, 1, 3, 2)).astype(ml_dtypes.float8_e4m3fn).view(np.uint8)
    return words, np.ascontiguousarray(byte.astype(np.uint8).reshape(k // 512, 16, n))


def unpack_weight(words, scales):
    g, p, n, _ = words.shape
    vals = np.ascontiguousarray(words).view(ml_dtypes.float8_e4m3fn).astype(np.float64) * np.repeat(np.exp2(scales.astype(np.float64) - 127.0), 8, axis=1)[..., None]
    return vals.transpose(0, 1, 3, 2).reshape(g * 512, n)


def sigmoid(v):
    return 1.0 / (1.0 + np.exp(-np.maximum(v, -700.0)))


K, T, S, G, H, C, U = 512, 1024, 256, 2048, 512, 512, 512


def setup_inputs():
    n = np.random.standard_normal
    s = mx_kscale(K)[:, None]
    packed_xT = pack_weight(n((K, T)) * s)
    packed_dT = pack_weight(n((K, G)) / s)
    perm = np.random.permutation(U)
    return {
        "x_words": packed_xT[0],
        "x_scales": packed_xT[1],
        "d_words": packed_dT[0],
        "d_scales": packed_dT[1],
        "sl": np.random.uniform(1.0, 2.0, (H, 1)).astype(np.float32),
        "th": (0.5 * n((H, 1))).astype(np.float32),
        "gs": (np.random.uniform(0.5, 1.5, (K, 1)) / s).astype(np.float32),
        "offs": striped(np.random.permutation(T)[:S]),
        "ka": striped8(np.random.randint(0, G, (8, H))),
        "kb": striped8(np.random.randint(0, G, (8, H))),
        "n1": striped8(np.stack([np.random.permutation(S) for _ in range(8)])),
        "n2": striped8(np.stack([np.random.permutation(S) for _ in range(8)])),
        "cand": striped(np.random.permutation(T)[:C]),
        "n3": striped(perm[:S]),
        "n4": striped(perm[S:]),
        "n5": striped(np.random.permutation(S)),
    }


def reference(x_words, x_scales, d_words, d_scales, sl, th, gs, offs, ka, kb, n1, n2, cand, n3, n4, n5):
    x_cand = unpack_weight(x_words, x_scales)[:, unstriped(cand)]
    d_ka = unpack_weight(d_words, d_scales)[np.arange(K)[:, None], runs(ka, K)]
    xq = unpack_weight(x_words, x_scales)[:, unstriped(offs)]
    d_kb = unpack_weight(d_words, d_scales)[np.arange(K)[:, None], runs(kb, K)]
    h = 0.0625 * (d_ka.T @ xq + d_kb.T @ xq)
    st = h - (h[np.arange(H)[:, None], runs(n1, H)])
    sg = sigmoid(f64(sl) * (st[np.arange(H)[:, None], runs(n2, H)] - f64(th)))
    z = f64(gs) * (h * sg)
    s = 0.0625 * ((x_cand.T @ mxq(z, 0, "e4m3")))
    nw = s - s[:, unstriped(n5)]
    ph = np.zeros((C, U))
    ph[:, unstriped(n3)] = s
    out = ph.copy()
    out[:, unstriped(n4)] = nw
    return out

@@ -1,0 +1,206 @@
+from contextlib import ExitStack
+
+import concourse.mybir as mybir
+from concourse.masks import make_identity
+
+K, T, S, G, H, C, U = 512, 1024, 256, 2048, 512, 512, 512
+FLOPS = 2 * K * S * (2 * H + C)
+
+F32 = mybir.dt.float32
+BF16 = mybir.dt.bfloat16
+I32 = mybir.dt.int32
+U32 = mybir.dt.uint32
+U16 = mybir.dt.uint16
+U8 = mybir.dt.uint8
+FP8X4 = mybir.dt.float8_e4m3fn_x4
+ACT = mybir.ActivationFunctionType
+ALU = mybir.AluOpType
+
+P = 128
+PACK = 4
+PER_COL = 16
+HALF = 256
+PIECES = ((0, 64), (64, 128), (128, 256))
+
+
+def entries(offsets, lo, hi):
+    return offsets[:, lo // PER_COL : hi // PER_COL]
+
+
+def tile_picked_aqcehqpagq_none_p_kernel(
+    tc, x_words, x_scales, d_words, d_scales, sl, th, gs, offs, ka, kb, n1, n2, cand, n3, n4, n5, out
+):
+    nc = tc.nc
+    with ExitStack() as ctx:
+        lists = ctx.enter_context(tc.tile_pool(name="lists", bufs=1))
+        keep = ctx.enter_context(tc.tile_pool(name="keep", bufs=1))
+        psum = ctx.enter_context(tc.psum_pool(name="psum", bufs=1))
+
+        def load_list(src, name):
+            tile = lists.tile(list(src.shape), U16, name=name)
+            nc.sync.dma_start(tile[:], src)
+            return tile
+
+        d_bytes = keep.tile([P, G], U8, align_bytes=64)
+        x_bytes = keep.tile([P, T], U8, align_bytes=64)
+        h_plane = keep.tile([P, 2 * H + S], U8, align_bytes=64)
+        cand_plane = keep.tile([P, C], U8, align_bytes=64)
+        nc.gpsimd.memset(d_bytes[:].bitcast(I32), 0)
+        nc.vector.memset(x_bytes[:].bitcast(I32), 0)
+        nc.vector.memset(h_plane[:].bitcast(I32), 0)
+        nc.vector.memset(cand_plane[:].bitcast(I32), 0)
+
+        def place_rows(queue, plane, picked):
+            for s in range(4):
+                queue.dma_start(plane[:].bitcast(I32)[s:P:32, :], picked[:].bitcast(I32)[8 * s : P : 32, :])
+
+        x_table = keep.tile([P, T], U32, align_bytes=64)
+        d_table = keep.tile([P, G], U32, align_bytes=64)
+        ka_l = load_list(ka, "ka_l")
+        kb_l = load_list(kb, "kb_l")
+        nc.sync.dma_start(d_bytes[:].bitcast(I32)[0:P:8, :], d_scales[0].bitcast(I32))
+        offs_l = load_list(offs, "offs_l")
+        n1_l = load_list(n1, "n1_l")
+        nc.sync.dma_start(x_bytes[:].bitcast(I32)[0:P:8, :], x_scales[0].bitcast(I32))
+        nc.sync.dma_start(x_table[:].bitcast(I32), x_words[0].rearrange("p n t -> p (n t)").bitcast(I32))
+        nc.sync.dma_start(d_table[:].bitcast(I32), d_words[0].rearrange("p n t -> p (n t)").bitcast(I32))
+        n2_l = load_list(n2, "n2_l")
+        cand_l = load_list(cand, "cand_l")
+        n3_l = load_list(n3, "n3_l")
+        n5_l = load_list(n5, "n5_l")
+        n4_l = load_list(n4, "n4_l")
+
+        slope = keep.tile([P, PACK], F32)
+        thresh = keep.tile([P, PACK], F32)
+        gain = keep.tile([P, PACK], F32)
+        for tile, src in ((slope, sl), (thresh, th), (gain, gs)):
+            nc.gpsimd.dma_start(tile[:], src.rearrange("(p t) o -> p (t o)", t=PACK))
+        ident = keep.tile([P, P], F32)
+        make_identity(nc, ident[:])
+
+        h_picked = keep.tile([P, 2 * H + S], U8, align_bytes=64)
+        for a, lst in enumerate((ka_l, kb_l)):
+            nc.vector.tensor_copy(h_picked[:, a * H : (a + 1) * H], d_bytes[:].indirect(lst[:]))
+        nc.vector.tensor_copy(h_picked[:, 2 * H :], x_bytes[:].indirect(offs_l[:]))
+        place_rows(nc.scalar, h_plane, h_picked)
+
+        xq_words = keep.tile([P, S], U32, align_bytes=64)
+        nc.vector.tensor_copy(xq_words[:], x_table[:].indirect(offs_l[:]))
+
+        bias = keep.tile([P, PACK], F32)
+        slope_thresh = keep.tile([P, PACK], F32)
+        nc.gpsimd.tensor_tensor(slope_thresh[:], slope[:], thresh[:], ALU.mult)
+        nc.gpsimd.tensor_scalar(bias[:], slope_thresh[:], -1.0, 0.0, ALU.mult, ALU.add)
+
+        ht_dealt = [keep.tile([P, PACK, P], F32, name=f"ht_dealt{u}") for u in range(2)]
+        for f in range(2):
+            banks = [psum.tile([P, HALF], F32, name=f"ht{u}{f}", tag=f"mx{u}{f}") for u in range(2)]
+            for a, lst in enumerate((ka_l, kb_l)):
+                words = keep.tile([P, HALF], U32, name=f"dw{a}{f}", tag=f"dw{a}{f}", align_bytes=64)
+                nc.vector.tensor_copy(words[:], d_table[:].indirect(entries(lst, f * HALF, (f + 1) * HALF)))
+                for u in range(2):
+                    nc.tensor.matmul_mx(
+                        out=banks[u][:],
+                        lhsT=xq_words[:, u * P : (u + 1) * P].bitcast(FP8X4),
+                        lhsT_scale=h_plane[:, 2 * H + u * P : 2 * H + (u + 1) * P],
+                        rhs=words[:].bitcast(FP8X4),
+                        rhs_scale=h_plane[:, a * H + f * HALF : a * H + (f + 1) * HALF],
+                        start=(a == 0),
+                        stop=(a == 1),
+                    )
+            for u in range(2):
+                nc.scalar.activation(
+                    out=ht_dealt[u][:, :, f * 64 : (f + 1) * 64],
+                    in_=banks[u][:].rearrange("p (m t) -> p t m", t=PACK),
+                    func=ACT.Copy,
+                    scale=0.0625,
+                )
+
+        cand_words = keep.tile([P, C], U32, tag="dw00", align_bytes=64)
+        cand_picked = keep.tile([P, C], U8, tag="dw10", align_bytes=64)
+        nc.vector.tensor_copy(cand_picked[:], x_bytes[:].indirect(cand_l[:]))
+        place_rows(nc.sync, cand_plane, cand_picked)
+        nc.vector.tensor_copy(cand_words[:], x_table[:].indirect(cand_l[:]))
+
+        h_banks = [psum.tile([P, S], F32, name=f"hb{t}", tag=f"hb{t}") for t in range(PACK)]
+        for t in range(PACK):
+            for u in range(2):
+                nc.tensor.transpose(h_banks[t][:, u * P : (u + 1) * P], ht_dealt[u][:, t, :], ident[:])
+
+        h = [keep.tile([P, S], F32, name=f"h{t}") for t in range(PACK)]
+        nc.scalar.copy(h[0][:], h_banks[0][:])
+        for t in range(1, PACK):
+            nc.vector.tensor_copy(h[t][:], h_banks[t][:])
+
+        st = [keep.tile([P, S], F32, name=f"st{t}") for t in range(PACK)]
+        for t in range(PACK):
+            h_n1 = keep.tile([P, S], F32, name=f"h_n1_{t}")
+            for lo in range(0, S, P):
+                nc.scalar.activation(
+                    out=h_n1[:, lo : lo + P], in_=h[t][:].indirect(entries(n1_l, lo, lo + P)), func=ACT.Copy
+                )
+            nc.vector.tensor_tensor(st[t][:], h[t][:], h_n1[:], ALU.subtract)
+
+        score = keep.tile([P, 4, S], F32)
+        for i, (lo, hi) in enumerate(PIECES):
+            width = hi - lo
+            z = keep.tile([P, width, PACK], BF16, name=f"z{i}", tag="z_words0" if i == 2 else f"z{i}", align_bytes=64)
+            if i == 1:
+                sg_rest = keep.tile([P, PACK, S - lo], F32, tag="sg2")
+            for t in range(PACK):
+                if i == 0:
+                    sg = keep.tile([P, width], F32, name=f"sg{t}", tag=f"sg{t}")[:]
+                else:
+                    sg = sg_rest[:, t, lo - PIECES[1][0] : hi - PIECES[1][0]]
+                nc.scalar.activation(
+                    out=sg,
+                    in_=st[t][:].indirect(entries(n2_l, lo, hi)),
+                    func=ACT.Sigmoid,
+                    scale=slope[:, t : t + 1],
+                    bias=bias[:, t : t + 1],
+                )
+                nc.vector.scalar_tensor_tensor(
+                    z[:, :, t], h[t][:, lo:hi], gain[:, t : t + 1], sg, ALU.mult, ALU.mult
+                )
+            z_words = keep.tile([P, width], U32, name=f"z_words{i}", tag=f"z_words{i}", align_bytes=64)
+            z_scales = keep.tile([P, width], U8, name=f"z_scales{i}", align_bytes=64)
+            nc.vector.quantize_mx(
+                out=z_words[:].bitcast(FP8X4), scales=z_scales[:], in_=z[:].rearrange("p w t -> p (w t)")
+            )
+            s_bank = psum.tile([P, 4, width], F32, name=f"s_bank{i}", tag=f"mx{i % 2}{i // 2}")
+            for c in range(4):
+                nc.tensor.matmul_mx(
+                    out=s_bank[:, c, :],
+                    lhsT=cand_words[:, c * P : (c + 1) * P].bitcast(FP8X4),
+                    lhsT_scale=cand_plane[:, c * P : (c + 1) * P],
+                    rhs=z_words[:].bitcast(FP8X4),
+                    rhs_scale=z_scales[:],
+                    start=True,
+                    stop=True,
+                )
+            nc.vector.tensor_scalar(score[:, :, lo:hi], s_bank[:], 0.0625, None, ALU.mult)
+
+        pages = [keep.tile([P, U], F32, name=f"page{c}") for c in range(4)]
+
+        def put_scores(c, lo, hi):
+            nc.scalar.activation(
+                out=pages[c][:].indirect(entries(n3_l, lo, hi)), in_=score[:, c, lo:hi], func=ACT.Copy
+            )
+
+        def put_differences(c, nw):
+            nc.scalar.activation(out=pages[c][:].indirect(n4_l[:]), in_=nw[:], func=ACT.Copy)
+            nc.sync.dma_start(out[c * P : (c + 1) * P, :], pages[c][:])
+
+        for lo, hi in PIECES[:-1]:
+            for c in range(4):
+                put_scores(c, lo, hi)
+        for c in range(4):
+            s_n5 = keep.tile([P, S], F32, name=f"s_n5_{c}")
+            for lo in range(0, S, P):
+                nc.scalar.activation(
+                    out=s_n5[:, lo : lo + P], in_=score[:, c, :].indirect(entries(n5_l, lo, lo + P)), func=ACT.Copy
+                )
+            nw = keep.tile([P, S], F32, name=f"nw{c}")
+            nc.vector.tensor_tensor(nw[:], score[:, c, :], s_n5[:], ALU.subtract)
+            put_scores(c, *PIECES[-1])
+            put_differences(c, nw)

@@ -77,6 +77,8 @@ def tile_picked_aqcehqpagq_none_p_kernel(
             nc.gpsimd.dma_start(tile[:], src.rearrange("(p t) o -> p (t o)", t=PACK))
         ident = keep.tile([P, P], F32)
         make_identity(nc, ident[:])
+        warm = keep.tile([P, 1], F32)
+        nc.scalar.activation(out=warm[:], in_=ident[:, 0:1], func=ACT.Sigmoid)
 
         h_picked = keep.tile([P, 2 * H + S], U8, align_bytes=64)
         for a, lst in enumerate((ka_l, kb_l)):

@@ -20,7 +20,7 @@ P = 128
 PACK = 4
 PER_COL = 16
 HALF = 256
-PIECES = ((0, 64), (64, 128), (128, 256))
+PIECES = ((0, 64), (64, 128), (128, 192), (192, 256))
 
 
 def entries(offsets, lo, hi):
@@ -43,27 +43,33 @@ def tile_picked_aqcehqpagq_none_p_kernel(
 
         d_bytes = keep.tile([P, G], U8, align_bytes=64)
         x_bytes = keep.tile([P, T], U8, align_bytes=64)
-        h_plane = keep.tile([P, 2 * H + S], U8, align_bytes=64)
-        cand_plane = keep.tile([P, C], U8, align_bytes=64)
+        h_plane = keep.tile([P, 2 * H], U8, align_bytes=64)
         nc.gpsimd.memset(d_bytes[:].bitcast(I32), 0)
+        ident = keep.tile([P, P], F32)
+        make_identity(nc, ident[:])
         nc.vector.memset(x_bytes[:].bitcast(I32), 0)
         nc.vector.memset(h_plane[:].bitcast(I32), 0)
-        nc.vector.memset(cand_plane[:].bitcast(I32), 0)
 
         def place_rows(queue, plane, picked):
             for s in range(4):
                 queue.dma_start(plane[:].bitcast(I32)[s:P:32, :], picked[:].bitcast(I32)[8 * s : P : 32, :])
 
+        warm = keep.tile([P, 2], F32)
+        nc.vector.memset(warm[:, 0:1], 0.0)
+        nc.scalar.activation(out=warm[:, 1:2], in_=warm[:, 0:1], func=ACT.Sigmoid)
         x_table = keep.tile([P, T], U32, align_bytes=64)
         d_table = keep.tile([P, G], U32, align_bytes=64)
         ka_l = load_list(ka, "ka_l")
         kb_l = load_list(kb, "kb_l")
         nc.sync.dma_start(d_bytes[:].bitcast(I32)[0:P:8, :], d_scales[0].bitcast(I32))
         offs_l = load_list(offs, "offs_l")
-        n1_l = load_list(n1, "n1_l")
-        nc.sync.dma_start(x_bytes[:].bitcast(I32)[0:P:8, :], x_scales[0].bitcast(I32))
+        for q in range(4):
+            nc.scalar.dma_start(
+                x_bytes[:].bitcast(I32)[32 * q : 32 * q + 4, :], x_scales[0].bitcast(I32)[4 * q : 4 * q + 4, :]
+            )
         nc.sync.dma_start(x_table[:].bitcast(I32), x_words[0].rearrange("p n t -> p (n t)").bitcast(I32))
         nc.sync.dma_start(d_table[:].bitcast(I32), d_words[0].rearrange("p n t -> p (n t)").bitcast(I32))
+        n1_l = load_list(n1, "n1_l")
         n2_l = load_list(n2, "n2_l")
         cand_l = load_list(cand, "cand_l")
         n3_l = load_list(n3, "n3_l")
@@ -75,16 +81,18 @@ def tile_picked_aqcehqpagq_none_p_kernel(
         gain = keep.tile([P, PACK], F32)
         for tile, src in ((slope, sl), (thresh, th), (gain, gs)):
             nc.gpsimd.dma_start(tile[:], src.rearrange("(p t) o -> p (t o)", t=PACK))
-        ident = keep.tile([P, P], F32)
-        make_identity(nc, ident[:])
-        warm = keep.tile([P, 1], F32)
-        nc.scalar.activation(out=warm[:], in_=ident[:, 0:1], func=ACT.Sigmoid)
 
-        h_picked = keep.tile([P, 2 * H + S], U8, align_bytes=64)
+        h = [keep.tile([P, 2 * S], F32, name=f"h{t}") for t in range(PACK)]
+        score = [keep.tile([P, S + PER_COL], F32, name=f"score{c}") for c in range(4)]
+        for tile in h + score:
+            nc.vector.memset(tile[:, S:], 0.0)
+
+        h_picked = keep.tile([P, 2 * H], U8, align_bytes=64)
         for a, lst in enumerate((ka_l, kb_l)):
             nc.vector.tensor_copy(h_picked[:, a * H : (a + 1) * H], d_bytes[:].indirect(lst[:]))
-        nc.vector.tensor_copy(h_picked[:, 2 * H :], x_bytes[:].indirect(offs_l[:]))
         place_rows(nc.scalar, h_plane, h_picked)
+        xq_scales = keep.tile([P, S], U8, align_bytes=64)
+        nc.vector.tensor_copy(xq_scales[:], x_bytes[:].indirect(offs_l[:]))
 
         xq_words = keep.tile([P, S], U32, align_bytes=64)
         nc.vector.tensor_copy(xq_words[:], x_table[:].indirect(offs_l[:]))
@@ -104,7 +112,7 @@ def tile_picked_aqcehqpagq_none_p_kernel(
                     nc.tensor.matmul_mx(
                         out=banks[u][:],
                         lhsT=xq_words[:, u * P : (u + 1) * P].bitcast(FP8X4),
-                        lhsT_scale=h_plane[:, 2 * H + u * P : 2 * H + (u + 1) * P],
+                        lhsT_scale=xq_scales[:, u * P : (u + 1) * P],
                         rhs=words[:].bitcast(FP8X4),
                         rhs_scale=h_plane[:, a * H + f * HALF : a * H + (f + 1) * HALF],
                         start=(a == 0),
@@ -121,7 +129,6 @@ def tile_picked_aqcehqpagq_none_p_kernel(
         cand_words = keep.tile([P, C], U32, tag="dw00", align_bytes=64)
         cand_picked = keep.tile([P, C], U8, tag="dw10", align_bytes=64)
         nc.vector.tensor_copy(cand_picked[:], x_bytes[:].indirect(cand_l[:]))
-        place_rows(nc.sync, cand_plane, cand_picked)
         nc.vector.tensor_copy(cand_words[:], x_table[:].indirect(cand_l[:]))
 
         h_banks = [psum.tile([P, S], F32, name=f"hb{t}", tag=f"hb{t}") for t in range(PACK)]
@@ -129,64 +136,76 @@ def tile_picked_aqcehqpagq_none_p_kernel(
             for u in range(2):
                 nc.tensor.transpose(h_banks[t][:, u * P : (u + 1) * P], ht_dealt[u][:, t, :], ident[:])
 
-        h = [keep.tile([P, S], F32, name=f"h{t}") for t in range(PACK)]
-        nc.scalar.copy(h[0][:], h_banks[0][:])
+        nc.scalar.copy(h[0][:, :S], h_banks[0][:])
         for t in range(1, PACK):
-            nc.vector.tensor_copy(h[t][:], h_banks[t][:])
+            nc.vector.tensor_copy(h[t][:, :S], h_banks[t][:])
 
         st = [keep.tile([P, S], F32, name=f"st{t}") for t in range(PACK)]
         for t in range(PACK):
             h_n1 = keep.tile([P, S], F32, name=f"h_n1_{t}")
-            for lo in range(0, S, P):
-                nc.scalar.activation(
-                    out=h_n1[:, lo : lo + P], in_=h[t][:].indirect(entries(n1_l, lo, lo + P)), func=ACT.Copy
-                )
-            nc.vector.tensor_tensor(st[t][:], h[t][:], h_n1[:], ALU.subtract)
+            nc.scalar.activation(out=h_n1[:], in_=h[t][:].indirect(n1_l[:]), func=ACT.Copy)
+            nc.vector.tensor_tensor(st[t][:], h[t][:, :S], h_n1[:], ALU.subtract)
 
-        score = keep.tile([P, 4, S], F32)
         for i, (lo, hi) in enumerate(PIECES):
             width = hi - lo
-            z = keep.tile([P, width, PACK], BF16, name=f"z{i}", tag="z_words0" if i == 2 else f"z{i}", align_bytes=64)
+            z = keep.tile([P, width, PACK], BF16, name=f"z{i}", align_bytes=64)
             if i == 1:
                 sg_rest = keep.tile([P, PACK, S - lo], F32, tag="sg2")
+            if i > 0:
+                z_rows = keep.tile(
+                    [P, PACK, width], BF16, name=f"z_rows{i}", tag=f"z_words{i - 2}" if i >= 2 else "z_rows1", align_bytes=64
+                )
             for t in range(PACK):
                 if i == 0:
                     sg = keep.tile([P, width], F32, name=f"sg{t}", tag=f"sg{t}")[:]
                 else:
                     sg = sg_rest[:, t, lo - PIECES[1][0] : hi - PIECES[1][0]]
-                nc.scalar.activation(
-                    out=sg,
-                    in_=st[t][:].indirect(entries(n2_l, lo, hi)),
-                    func=ACT.Sigmoid,
-                    scale=slope[:, t : t + 1],
-                    bias=bias[:, t : t + 1],
-                )
+                if i < 3:
+                    end = hi if i < 2 else S
+                    nc.scalar.activation(
+                        out=sg if i < 2 else sg_rest[:, t, lo - PIECES[1][0] :],
+                        in_=st[t][:].indirect(entries(n2_l, lo, end)),
+                        func=ACT.Sigmoid,
+                        scale=slope[:, t : t + 1],
+                        bias=bias[:, t : t + 1],
+                    )
                 nc.vector.scalar_tensor_tensor(
-                    z[:, :, t], h[t][:, lo:hi], gain[:, t : t + 1], sg, ALU.mult, ALU.mult
+                    z[:, :, t] if i == 0 else z_rows[:, t, :],
+                    h[t][:, lo:hi],
+                    gain[:, t : t + 1],
+                    sg,
+                    ALU.mult,
+                    ALU.mult,
+                )
+            if i > 0:
+                nc.vector.tensor_copy(
+                    z[:].rearrange("p (c e) t -> p c t e", e=4), z_rows[:].rearrange("p t (c e) -> p c t e", e=4)
                 )
             z_words = keep.tile([P, width], U32, name=f"z_words{i}", tag=f"z_words{i}", align_bytes=64)
             z_scales = keep.tile([P, width], U8, name=f"z_scales{i}", align_bytes=64)
             nc.vector.quantize_mx(
                 out=z_words[:].bitcast(FP8X4), scales=z_scales[:], in_=z[:].rearrange("p w t -> p (w t)")
             )
-            s_bank = psum.tile([P, 4, width], F32, name=f"s_bank{i}", tag=f"mx{i % 2}{i // 2}")
             for c in range(4):
+                bank = psum.tile(
+                    [P, width], F32, name=f"s_bank{i}{c}", tag=f"mx{c % 2}{c // 2}" if i % 2 == 0 else f"hb{c}"
+                )
                 nc.tensor.matmul_mx(
-                    out=s_bank[:, c, :],
+                    out=bank[:],
                     lhsT=cand_words[:, c * P : (c + 1) * P].bitcast(FP8X4),
-                    lhsT_scale=cand_plane[:, c * P : (c + 1) * P],
+                    lhsT_scale=cand_picked[:, c * P : (c + 1) * P],
                     rhs=z_words[:].bitcast(FP8X4),
                     rhs_scale=z_scales[:],
                     start=True,
                     stop=True,
                 )
-            nc.vector.tensor_scalar(score[:, :, lo:hi], s_bank[:], 0.0625, None, ALU.mult)
+                nc.vector.tensor_scalar(score[c][:, lo:hi], bank[:], 0.0625, None, ALU.mult)
 
         pages = [keep.tile([P, U], F32, name=f"page{c}") for c in range(4)]
 
         def put_scores(c, lo, hi):
             nc.scalar.activation(
-                out=pages[c][:].indirect(entries(n3_l, lo, hi)), in_=score[:, c, lo:hi], func=ACT.Copy
+                out=pages[c][:].indirect(entries(n3_l, lo, hi)), in_=score[c][:, lo:hi], func=ACT.Copy
             )
 
         def put_differences(c, nw):
@@ -198,11 +217,8 @@ def tile_picked_aqcehqpagq_none_p_kernel(
                 put_scores(c, lo, hi)
         for c in range(4):
             s_n5 = keep.tile([P, S], F32, name=f"s_n5_{c}")
-            for lo in range(0, S, P):
-                nc.scalar.activation(
-                    out=s_n5[:, lo : lo + P], in_=score[:, c, :].indirect(entries(n5_l, lo, lo + P)), func=ACT.Copy
-                )
+            nc.scalar.activation(out=s_n5[:], in_=score[c][:].indirect(n5_l[:]), func=ACT.Copy)
             nw = keep.tile([P, S], F32, name=f"nw{c}")
-            nc.vector.tensor_tensor(nw[:], score[:, c, :], s_n5[:], ALU.subtract)
+            nc.vector.tensor_tensor(nw[:], score[c][:, :S], s_n5[:], ALU.subtract)
             put_scores(c, *PIECES[-1])
             put_differences(c, nw)

@@ -1,7 +1,6 @@
 from contextlib import ExitStack
 
 import concourse.mybir as mybir
-from concourse.masks import make_identity
 
 K, T, S, G, H, C, U = 512, 1024, 256, 2048, 512, 512, 512
 FLOPS = 2 * K * S * (2 * H + C)
@@ -45,8 +44,6 @@ def tile_picked_aqcehqpagq_none_p_kernel(
         x_bytes = keep.tile([P, T], U8, align_bytes=64)
         h_plane = keep.tile([P, 2 * H], U8, align_bytes=64)
         nc.gpsimd.memset(d_bytes[:].bitcast(I32), 0)
-        ident = keep.tile([P, P], F32)
-        make_identity(nc, ident[:])
         nc.vector.memset(x_bytes[:].bitcast(I32), 0)
         nc.vector.memset(h_plane[:].bitcast(I32), 0)
 
@@ -90,7 +87,12 @@ def tile_picked_aqcehqpagq_none_p_kernel(
         h_picked = keep.tile([P, 2 * H], U8, align_bytes=64)
         for a, lst in enumerate((ka_l, kb_l)):
             nc.vector.tensor_copy(h_picked[:, a * H : (a + 1) * H], d_bytes[:].indirect(lst[:]))
-        place_rows(nc.scalar, h_plane, h_picked)
+        h_dealt = keep.tile([P, 2 * H], U8, align_bytes=64)
+        nc.vector.tensor_copy(
+            h_dealt[:].rearrange("p (a t m) -> p a t m", a=2, t=PACK),
+            h_picked[:].rearrange("p (a m t) -> p a t m", a=2, t=PACK),
+        )
+        place_rows(nc.scalar, h_plane, h_dealt)
         xq_scales = keep.tile([P, S], U8, align_bytes=64)
         nc.vector.tensor_copy(xq_scales[:], x_bytes[:].indirect(offs_l[:]))
 
@@ -102,43 +104,42 @@ def tile_picked_aqcehqpagq_none_p_kernel(
         nc.gpsimd.tensor_tensor(slope_thresh[:], slope[:], thresh[:], ALU.mult)
         nc.gpsimd.tensor_scalar(bias[:], slope_thresh[:], -1.0, 0.0, ALU.mult, ALU.add)
 
-        ht_dealt = [keep.tile([P, PACK, P], F32, name=f"ht_dealt{u}") for u in range(2)]
-        for f in range(2):
-            banks = [psum.tile([P, HALF], F32, name=f"ht{u}{f}", tag=f"mx{u}{f}") for u in range(2)]
-            for a, lst in enumerate((ka_l, kb_l)):
-                words = keep.tile([P, HALF], U32, name=f"dw{a}{f}", tag=f"dw{a}{f}", align_bytes=64)
-                nc.vector.tensor_copy(words[:], d_table[:].indirect(entries(lst, f * HALF, (f + 1) * HALF)))
-                for u in range(2):
-                    nc.tensor.matmul_mx(
-                        out=banks[u][:],
-                        lhsT=xq_words[:, u * P : (u + 1) * P].bitcast(FP8X4),
-                        lhsT_scale=xq_scales[:, u * P : (u + 1) * P],
-                        rhs=words[:].bitcast(FP8X4),
-                        rhs_scale=h_plane[:, a * H + f * HALF : a * H + (f + 1) * HALF],
-                        start=(a == 0),
-                        stop=(a == 1),
-                    )
-            for u in range(2):
-                nc.scalar.activation(
-                    out=ht_dealt[u][:, :, f * 64 : (f + 1) * 64],
-                    in_=banks[u][:].rearrange("p (m t) -> p t m", t=PACK),
-                    func=ACT.Copy,
-                    scale=0.0625,
-                )
+        d_picked = []
+        for a, lst in enumerate((ka_l, kb_l)):
+            words = keep.tile([P, H], U32, name=f"d_picked{a}", tag=f"d_picked{a}", align_bytes=64)
+            nc.vector.tensor_copy(words[:], d_table[:].indirect(lst[:]))
+            d_picked.append(words)
+        d_dealt = []
+        for a, words in enumerate(d_picked):
+            dealt = keep.tile([P, H], U32, name=f"d_dealt{a}", tag=f"d_dealt{a}", align_bytes=64)
+            nc.vector.tensor_copy(
+                dealt[:].rearrange("p (t c e) -> p c t e", t=PACK, e=4),
+                words[:].rearrange("p (c e t) -> p c t e", t=PACK, e=4),
+            )
+            d_dealt.append(dealt)
 
-        cand_words = keep.tile([P, C], U32, tag="dw00", align_bytes=64)
-        cand_picked = keep.tile([P, C], U8, tag="dw10", align_bytes=64)
+        cand_picked = keep.tile([P, C], U8, tag="d_picked1", align_bytes=64)
         nc.vector.tensor_copy(cand_picked[:], x_bytes[:].indirect(cand_l[:]))
-        nc.vector.tensor_copy(cand_words[:], x_table[:].indirect(cand_l[:]))
 
-        h_banks = [psum.tile([P, S], F32, name=f"hb{t}", tag=f"hb{t}") for t in range(PACK)]
         for t in range(PACK):
-            for u in range(2):
-                nc.tensor.transpose(h_banks[t][:, u * P : (u + 1) * P], ht_dealt[u][:, t, :], ident[:])
+            h_bank = psum.tile([P, S], F32, name=f"h_bank{t}", tag=f"hb{t}")
+            for a in range(2):
+                nc.tensor.matmul_mx(
+                    out=h_bank[:],
+                    lhsT=d_dealt[a][:, t * P : (t + 1) * P].bitcast(FP8X4),
+                    lhsT_scale=h_plane[:, a * H + t * P : a * H + (t + 1) * P],
+                    rhs=xq_words[:].bitcast(FP8X4),
+                    rhs_scale=xq_scales[:],
+                    start=(a == 0),
+                    stop=(a == 1),
+                )
+            if t == 0:
+                nc.scalar.activation(out=h[t][:, :S], in_=h_bank[:], func=ACT.Copy, scale=0.0625)
+            else:
+                nc.vector.tensor_scalar(h[t][:, :S], h_bank[:], 0.0625, None, ALU.mult)
 
-        nc.scalar.copy(h[0][:, :S], h_banks[0][:])
-        for t in range(1, PACK):
-            nc.vector.tensor_copy(h[t][:, :S], h_banks[t][:])
+        cand_words = keep.tile([P, C], U32, tag="d_dealt1", align_bytes=64)
+        nc.vector.tensor_copy(cand_words[:], x_table[:].indirect(cand_l[:]))
 
         st = [keep.tile([P, S], F32, name=f"st{t}") for t in range(PACK)]
         for t in range(PACK):

from contextlib import ExitStack

import concourse.mybir as mybir

K, T, S, G, H, C, U = 512, 1024, 256, 2048, 512, 512, 512
FLOPS = 2 * K * S * (2 * H + C)

F32 = mybir.dt.float32
BF16 = mybir.dt.bfloat16
I32 = mybir.dt.int32
U32 = mybir.dt.uint32
U16 = mybir.dt.uint16
U8 = mybir.dt.uint8
FP8X4 = mybir.dt.float8_e4m3fn_x4
ACT = mybir.ActivationFunctionType
ALU = mybir.AluOpType

P = 128
PACK = 4
PER_COL = 16
HALF = 256
PIECES = ((0, 64), (64, 128), (128, 192), (192, 256))


def entries(offsets, lo, hi):
    return offsets[:, lo // PER_COL : hi // PER_COL]


def tile_picked_aqcehqpagq_none_p_kernel(
    tc, x_words, x_scales, d_words, d_scales, sl, th, gs, offs, ka, kb, n1, n2, cand, n3, n4, n5, out
):
    nc = tc.nc
    with ExitStack() as ctx:
        lists = ctx.enter_context(tc.tile_pool(name="lists", bufs=1))
        keep = ctx.enter_context(tc.tile_pool(name="keep", bufs=1))
        psum = ctx.enter_context(tc.psum_pool(name="psum", bufs=1))

        def load_list(src, name):
            tile = lists.tile(list(src.shape), U16, name=name)
            nc.sync.dma_start(tile[:], src)
            return tile

        d_bytes = keep.tile([P, G], U8, align_bytes=64)
        x_bytes = keep.tile([P, T], U8, align_bytes=64)
        h_plane = keep.tile([P, 2 * H], U8, align_bytes=64)
        nc.gpsimd.memset(d_bytes[:].bitcast(I32), 0)
        nc.vector.memset(x_bytes[:].bitcast(I32), 0)
        nc.vector.memset(h_plane[:].bitcast(I32), 0)

        def place_rows(queue, plane, picked):
            for s in range(4):
                queue.dma_start(plane[:].bitcast(I32)[s:P:32, :], picked[:].bitcast(I32)[8 * s : P : 32, :])

        warm = keep.tile([P, 2], F32)
        nc.vector.memset(warm[:, 0:1], 0.0)
        nc.scalar.activation(out=warm[:, 1:2], in_=warm[:, 0:1], func=ACT.Sigmoid)
        x_table = keep.tile([P, T], U32, align_bytes=64)
        d_table = keep.tile([P, G], U32, align_bytes=64)
        ka_l = load_list(ka, "ka_l")
        kb_l = load_list(kb, "kb_l")
        nc.sync.dma_start(d_bytes[:].bitcast(I32)[0:P:8, :], d_scales[0].bitcast(I32))
        offs_l = load_list(offs, "offs_l")
        for q in range(4):
            nc.scalar.dma_start(
                x_bytes[:].bitcast(I32)[32 * q : 32 * q + 4, :], x_scales[0].bitcast(I32)[4 * q : 4 * q + 4, :]
            )
        nc.sync.dma_start(x_table[:].bitcast(I32), x_words[0].rearrange("p n t -> p (n t)").bitcast(I32))
        nc.sync.dma_start(d_table[:].bitcast(I32), d_words[0].rearrange("p n t -> p (n t)").bitcast(I32))
        n1_l = load_list(n1, "n1_l")
        n2_l = load_list(n2, "n2_l")
        cand_l = load_list(cand, "cand_l")
        n3_l = load_list(n3, "n3_l")
        n5_l = load_list(n5, "n5_l")
        n4_l = load_list(n4, "n4_l")

        slope = keep.tile([P, PACK], F32)
        thresh = keep.tile([P, PACK], F32)
        gain = keep.tile([P, PACK], F32)
        for tile, src in ((slope, sl), (thresh, th), (gain, gs)):
            nc.gpsimd.dma_start(tile[:], src.rearrange("(p t) o -> p (t o)", t=PACK))

        h = [keep.tile([P, 2 * S], F32, name=f"h{t}") for t in range(PACK)]
        score = [keep.tile([P, S + PER_COL], F32, name=f"score{c}") for c in range(4)]
        for tile in h + score:
            nc.vector.memset(tile[:, S:], 0.0)

        h_picked = keep.tile([P, 2 * H], U8, align_bytes=64)
        for a, lst in enumerate((ka_l, kb_l)):
            nc.vector.tensor_copy(h_picked[:, a * H : (a + 1) * H], d_bytes[:].indirect(lst[:]))
        h_dealt = keep.tile([P, 2 * H], U8, align_bytes=64)
        nc.vector.tensor_copy(
            h_dealt[:].rearrange("p (a t m) -> p a t m", a=2, t=PACK),
            h_picked[:].rearrange("p (a m t) -> p a t m", a=2, t=PACK),
        )
        place_rows(nc.scalar, h_plane, h_dealt)
        xq_scales = keep.tile([P, S], U8, align_bytes=64)
        nc.vector.tensor_copy(xq_scales[:], x_bytes[:].indirect(offs_l[:]))

        xq_words = keep.tile([P, S], U32, align_bytes=64)
        nc.vector.tensor_copy(xq_words[:], x_table[:].indirect(offs_l[:]))

        bias = keep.tile([P, PACK], F32)
        slope_thresh = keep.tile([P, PACK], F32)
        nc.gpsimd.tensor_tensor(slope_thresh[:], slope[:], thresh[:], ALU.mult)
        nc.gpsimd.tensor_scalar(bias[:], slope_thresh[:], -1.0, 0.0, ALU.mult, ALU.add)

        d_picked = []
        for a, lst in enumerate((ka_l, kb_l)):
            words = keep.tile([P, H], U32, name=f"d_picked{a}", tag=f"d_picked{a}", align_bytes=64)
            nc.vector.tensor_copy(words[:], d_table[:].indirect(lst[:]))
            d_picked.append(words)
        d_dealt = []
        for a, words in enumerate(d_picked):
            dealt = keep.tile([P, H], U32, name=f"d_dealt{a}", tag=f"d_dealt{a}", align_bytes=64)
            nc.vector.tensor_copy(
                dealt[:].rearrange("p (t c e) -> p c t e", t=PACK, e=4),
                words[:].rearrange("p (c e t) -> p c t e", t=PACK, e=4),
            )
            d_dealt.append(dealt)

        cand_picked = keep.tile([P, C], U8, tag="d_picked1", align_bytes=64)
        nc.vector.tensor_copy(cand_picked[:], x_bytes[:].indirect(cand_l[:]))

        for t in range(PACK):
            h_bank = psum.tile([P, S], F32, name=f"h_bank{t}", tag=f"hb{t}")
            for a in range(2):
                nc.tensor.matmul_mx(
                    out=h_bank[:],
                    lhsT=d_dealt[a][:, t * P : (t + 1) * P].bitcast(FP8X4),
                    lhsT_scale=h_plane[:, a * H + t * P : a * H + (t + 1) * P],
                    rhs=xq_words[:].bitcast(FP8X4),
                    rhs_scale=xq_scales[:],
                    start=(a == 0),
                    stop=(a == 1),
                )
            if t == 0:
                nc.scalar.activation(out=h[t][:, :S], in_=h_bank[:], func=ACT.Copy, scale=0.0625)
            else:
                nc.vector.tensor_scalar(h[t][:, :S], h_bank[:], 0.0625, None, ALU.mult)

        cand_words = keep.tile([P, C], U32, tag="d_dealt1", align_bytes=64)
        nc.vector.tensor_copy(cand_words[:], x_table[:].indirect(cand_l[:]))

        st = [keep.tile([P, S], F32, name=f"st{t}") for t in range(PACK)]
        for t in range(PACK):
            h_n1 = keep.tile([P, S], F32, name=f"h_n1_{t}")
            nc.scalar.activation(out=h_n1[:], in_=h[t][:].indirect(n1_l[:]), func=ACT.Copy)
            nc.vector.tensor_tensor(st[t][:], h[t][:, :S], h_n1[:], ALU.subtract)

        for i, (lo, hi) in enumerate(PIECES):
            width = hi - lo
            z = keep.tile([P, width, PACK], BF16, name=f"z{i}", align_bytes=64)
            if i == 1:
                sg_rest = keep.tile([P, PACK, S - lo], F32, tag="sg2")
            if i > 0:
                z_rows = keep.tile(
                    [P, PACK, width], BF16, name=f"z_rows{i}", tag=f"z_words{i - 2}" if i >= 2 else "z_rows1", align_bytes=64
                )
            for t in range(PACK):
                if i == 0:
                    sg = keep.tile([P, width], F32, name=f"sg{t}", tag=f"sg{t}")[:]
                else:
                    sg = sg_rest[:, t, lo - PIECES[1][0] : hi - PIECES[1][0]]
                if i < 3:
                    end = hi if i < 2 else S
                    nc.scalar.activation(
                        out=sg if i < 2 else sg_rest[:, t, lo - PIECES[1][0] :],
                        in_=st[t][:].indirect(entries(n2_l, lo, end)),
                        func=ACT.Sigmoid,
                        scale=slope[:, t : t + 1],
                        bias=bias[:, t : t + 1],
                    )
                nc.vector.scalar_tensor_tensor(
                    z[:, :, t] if i == 0 else z_rows[:, t, :],
                    h[t][:, lo:hi],
                    gain[:, t : t + 1],
                    sg,
                    ALU.mult,
                    ALU.mult,
                )
            if i > 0:
                nc.vector.tensor_copy(
                    z[:].rearrange("p (c e) t -> p c t e", e=4), z_rows[:].rearrange("p t (c e) -> p c t e", e=4)
                )
            z_words = keep.tile([P, width], U32, name=f"z_words{i}", tag=f"z_words{i}", align_bytes=64)
            z_scales = keep.tile([P, width], U8, name=f"z_scales{i}", align_bytes=64)
            nc.vector.quantize_mx(
                out=z_words[:].bitcast(FP8X4), scales=z_scales[:], in_=z[:].rearrange("p w t -> p (w t)")
            )
            for c in range(4):
                bank = psum.tile(
                    [P, width], F32, name=f"s_bank{i}{c}", tag=f"mx{c % 2}{c // 2}" if i % 2 == 0 else f"hb{c}"
                )
                nc.tensor.matmul_mx(
                    out=bank[:],
                    lhsT=cand_words[:, c * P : (c + 1) * P].bitcast(FP8X4),
                    lhsT_scale=cand_picked[:, c * P : (c + 1) * P],
                    rhs=z_words[:].bitcast(FP8X4),
                    rhs_scale=z_scales[:],
                    start=True,
                    stop=True,
                )
                nc.vector.tensor_scalar(score[c][:, lo:hi], bank[:], 0.0625, None, ALU.mult)

        pages = [keep.tile([P, U], F32, name=f"page{c}") for c in range(4)]

        def put_scores(c, lo, hi):
            nc.scalar.activation(
                out=pages[c][:].indirect(entries(n3_l, lo, hi)), in_=score[c][:, lo:hi], func=ACT.Copy
            )

        def put_differences(c, nw):
            nc.scalar.activation(out=pages[c][:].indirect(n4_l[:]), in_=nw[:], func=ACT.Copy)
            nc.sync.dma_start(out[c * P : (c + 1) * P, :], pages[c][:])

        for lo, hi in PIECES[:-1]:
            for c in range(4):
                put_scores(c, lo, hi)
        for c in range(4):
            s_n5 = keep.tile([P, S], F32, name=f"s_n5_{c}")
            nc.scalar.activation(out=s_n5[:], in_=score[c][:].indirect(n5_l[:]), func=ACT.Copy)
            nw = keep.tile([P, S], F32, name=f"nw{c}")
            nc.vector.tensor_tensor(nw[:], score[c][:, :S], s_n5[:], ALU.subtract)
            put_scores(c, *PIECES[-1])
            put_differences(c, nw)
